import numpy as np
import ml_dtypes


def mxq(x, axis, fmt="e4m3"):
    dtype, down = {"e4m3": (ml_dtypes.float8_e4m3fn, 7), "e5m2": (ml_dtypes.float8_e5m2, 14)}[fmt]
    v = np.moveaxis(np.asarray(x, np.float32).astype(ml_dtypes.bfloat16).astype(np.float64), axis, -1)
    blocks = v.reshape(v.shape[:-1] + (-1, 32))
    amax = np.abs(blocks).max(-1, keepdims=True)
    byte = np.maximum(np.where(amax > 0, np.frexp(amax)[1] - 1 + 127, 0) - down, 1)
    scale = np.exp2(byte - 127.0)
    codes = (blocks / scale).astype(np.float32).astype(dtype).astype(np.float64)
    return np.moveaxis((codes * scale).reshape(v.shape), -1, axis)


WIDE = False


def mx_kscale(k):
    if not WIDE:
        return np.ones(k)
    levels = np.array([30, -30])
    if k % 512:
        return np.exp2(np.random.permutation(np.resize(levels, k // 32))).repeat(32)
    a = np.empty((k // 512, 16))
    for p in range(k // 512):
        a[p, :8] = np.random.permutation(np.resize(levels, 8))
        for g in range(8):
            far = levels[np.abs(levels - a[p, g]) >= 10]
            a[p, g + 8] = far[np.random.randint(len(far))]
    return np.exp2(a.ravel()).repeat(32)


def f64(x):
    return np.asarray(x).astype(np.float64)


def striped(idx):
    return np.tile(np.asarray(idx).reshape(-1, 16).T, (8, 1)).astype(np.uint16)


def unstriped(offs):
    return offs[:16].T.reshape(-1).astype(np.int64)


E2M1 = np.array([0.0, 0.5, 1.0, 1.5, 2.0, 3.0, 4.0, 6.0, -0.0, -0.5, -1.0, -1.5, -2.0, -3.0, -4.0, -6.0])


def pack_weight(w, fmt):
    k, n = w.shape
    w = f64(np.asarray(w, np.float32).astype(ml_dtypes.bfloat16)).reshape(k // 32, 32, n)
    amax = np.abs(w).max(1)
    if fmt in ("e4m3", "e5m2"):
        byte = np.frexp(amax)[1] - 1 + 127 - (7 if fmt == "e4m3" else 14)
    else:
        mant, ex = np.frexp(amax / 6.0)
        byte = np.where(mant > 0.5, ex, ex - 1) + 127
    byte = np.clip(np.where(amax > 0, byte, 1), 1, 254)
    scaled = (w * np.exp2(127.0 - byte)[:, None, :]).reshape(k, n).astype(np.float32)
    by_word = np.ascontiguousarray(scaled.reshape(k // 512, 128, 4, n).transpose(0, 1, 3, 2))
    if fmt in ("e4m3", "e5m2"):
        words = by_word.astype(ml_dtypes.float8_e4m3fn if fmt == "e4m3" else ml_dtypes.float8_e5m2).view(np.uint8)
    else:
        c = by_word.astype(ml_dtypes.float4_e2m1fn).view(np.uint8) & 0xF
        words = (c[..., 0::2] | (c[..., 1::2] << 4)).reshape(k // 512, 128, 2 * n)
    return np.ascontiguousarray(words), np.ascontiguousarray(byte.astype(np.uint8).reshape(k // 512, 16, n))


def unpack_weight(words, scales, fmt):
    g, _, n = scales.shape
    words = np.ascontiguousarray(words).reshape(g, 128, n, -1)
    if fmt in ("e4m3", "e5m2"):
        vals = words.view(ml_dtypes.float8_e4m3fn if fmt == "e4m3" else ml_dtypes.float8_e5m2).astype(np.float64)
    else:
        nib = np.empty((g, 128, n, 4), np.uint8)
        nib[..., 0::2] = words & 0xF
        nib[..., 1::2] = words >> 4
        vals = E2M1[nib]
    vals = vals * np.repeat(np.exp2(scales.astype(np.float64) - 127.0), 8, axis=1)[..., None]
    return vals.transpose(0, 1, 3, 2).reshape(g * 512, n)


def e4m3fn_bytes(y):
    return np.clip(np.asarray(y, np.float64), -448.0, 448.0).astype(np.float32).astype(ml_dtypes.float8_e4m3fn).view(np.uint8)


def e4m3fn_values(b):
    return np.asarray(b, np.uint8).view(ml_dtypes.float8_e4m3fn).astype(np.float64)


K, T, J, R, U, V, E, N = 512, 1024, 256, 512, 128, 1024, 512, 256


def setup_inputs():
    n = np.random.standard_normal
    idx = np.random.permutation(T)[:J]
    idx2 = np.random.permutation(J)[:U]
    idx3 = np.random.permutation(V)[:U]
    idx4 = np.random.permutation(E)[:U]
    fk = mx_kscale(K)
    fr = mx_kscale(R)
    xtp = pack_weight(n((K, T)) / fk[:, None], "e2m1")
    wp = pack_weight(n((K, R)) * 1 / np.sqrt(K) * fk[:, None] * fr, "e4m3")
    w2p = pack_weight(n((K, R)) * 1 / np.sqrt(K) * fk[:, None] * fr, "e5m2")
    wbp = pack_weight(n((R, N)) * 1 / np.sqrt(R) / fr[:, None], "e2m1")
    return {
        "xt_words": xtp[0],
        "xt_scales": xtp[1],
        "w_words": wp[0],
        "w_scales": wp[1],
        "w2_words": w2p[0],
        "w2_scales": w2p[1],
        "wb_words": wbp[0],
        "wb_scales": wbp[1],
        "ca": e4m3fn_bytes(60.0 * n((N, V))),
        "sz": (np.random.uniform(0.004, 0.012, (N, 1))).astype(np.float32),
        "offs": striped(idx),
        "offs2": striped(idx2),
        "offs3": striped(idx3),
        "offs4": striped(idx4),
    }


def reference(xt_words, xt_scales, w_words, w_scales, w2_words, w2_scales, wb_words, wb_scales, ca, sz, offs, offs2, offs3, offs4):
    idx = unstriped(offs)
    idx2 = unstriped(offs2)
    idx3 = unstriped(offs3)
    idx4 = unstriped(offs4)
    xtu = unpack_weight(xt_words, xt_scales, "e2m1")
    wu = unpack_weight(w_words, w_scales, "e4m3")
    w2u = unpack_weight(w2_words, w2_scales, "e5m2")
    wbu = unpack_weight(wb_words, wb_scales, "e2m1")
    xtidxg = xtu[:, idx]
    a = wu.T @ xtidxg
    b = w2u.T @ xtidxg
    hid = np.maximum(a, b)
    hidq = mxq(hid, 0, "e5m2")
    p = wbu.T @ hidq
    g1 = e4m3fn_values(ca)[:, idx3] * f64(sz)
    m0 = p[:, idx2] * g1
    y = np.zeros((N, E))
    y[:, idx4] = m0
    return y

@@ -1,0 +1,178 @@
+from contextlib import ExitStack
+
+import concourse.mybir as mybir
+
+K, T, J, R, U, V, E, N = 512, 1024, 256, 512, 128, 1024, 512, 256
+FLOPS = 2 * (2 * K * R * J + R * N * J)
+
+F32 = mybir.dt.float32
+BF16 = mybir.dt.bfloat16
+I32 = mybir.dt.int32
+U32 = mybir.dt.uint32
+U16 = mybir.dt.uint16
+U8 = mybir.dt.uint8
+E4M3 = mybir.dt.float8_e4m3fn
+E4M3X4 = mybir.dt.float8_e4m3fn_x4
+E5M2X4 = mybir.dt.float8_e5m2_x4
+E2M1X4 = mybir.dt.float4_e2m1fn_x4
+MULT = mybir.AluOpType.mult
+MAX = mybir.AluOpType.max
+COPY = mybir.ActivationFunctionType.Copy
+
+P = 128
+PACK = 4
+QUADS = 4
+QUAD = 32
+ROWS = 4
+SLOTS = 128
+HALVES = 2
+
+
+def load_scale_rows(queue, plane, scales):
+    for q in range(QUADS):
+        queue.dma_start(
+            plane[QUAD * q : QUAD * q + ROWS, :].bitcast(I32),
+            scales[0, ROWS * q : ROWS * (q + 1), :].bitcast(I32),
+        )
+
+
+def tile_list_outcomegain_kernel(
+    tc, xt_words, xt_scales, w_words, w_scales, w2_words, w2_scales, wb_words, wb_scales,
+    ca, sz, offs, offs2, offs3, offs4, out,
+):
+    nc = tc.nc
+    with ExitStack() as ctx:
+        sb = ctx.enter_context(tc.tile_pool(name="sb", bufs=1))
+        ps = ctx.enter_context(tc.psum_pool(name="ps", bufs=1))
+
+        def tile(name, shape, dtype, tag=None):
+            return sb.tile(shape, dtype, name=name, tag=tag or name, align_bytes=64)
+
+        tok_list = tile("tok_list", [P, J // 16], U16)
+        slot_list = tile("slot_list", [P, U // 16], U16)
+        gain_list = tile("gain_list", [P, U // 16], U16)
+        page_list = tile("page_list", [P, U // 16], U16)
+        xw = tile("xw", [P, T], U16)
+        xs = tile("xs", [P, T], U8)
+        ww = tile("ww", [P, R], U32)
+        ws = tile("ws", [P, 2 * R], U8)
+        w2w = tile("w2w", [P, R], U32)
+        w2s = tile("w2s", [P, 2 * R], U8)
+        wbw = tile("wbw", [P, N], U16)
+        wbs = tile("wbs", [P, N], U8)
+        step = tile("step", [P, HALVES], F32)
+        store = [tile("store%d" % h, [P, V], U8) for h in range(HALVES)]
+        page = [tile("page%d" % h, [P, E], F32) for h in range(HALVES)]
+
+        for plane in (xs, ws, w2s, wbs):
+            nc.vector.memset(plane[:].bitcast(I32), 0)
+        for h in range(HALVES):
+            nc.vector.memset(page[h][:], 0.0)
+
+        def load_folded(plane, scales):
+            rows = scales[0].bitcast(I32).rearrange("(u q r) c -> q r u c", u=2, q=2)
+            for q in range(2):
+                nc.sync.dma_start(
+                    plane[:].bitcast(I32)[QUAD * q : QUAD * q + ROWS, :].rearrange("r (u c) -> r u c", u=2), rows[q]
+                )
+
+        load_scale_rows(nc.scalar, xs, xt_scales)
+        nc.sync.dma_start(tok_list[:], offs)
+        nc.sync.dma_start(xw[:].bitcast(I32), xt_words[0].bitcast(I32))
+        nc.sync.dma_start(ww[:].bitcast(I32), w_words[0].rearrange("p c t -> p (c t)").bitcast(I32))
+        load_folded(ws, w_scales)
+        nc.sync.dma_start(w2w[:].bitcast(I32), w2_words[0].rearrange("p c t -> p (c t)").bitcast(I32))
+        load_folded(w2s, w2_scales)
+        nc.sync.dma_start(gain_list[:], offs3)
+        for h in range(HALVES):
+            nc.sync.dma_start(store[h][:], ca[P * h : P * (h + 1), :])
+        with nc.allow_non_contiguous_dma(reason="one float32 step for each partition and half"):
+            nc.sync.dma_start(step[:], sz.rearrange("(h p) o -> p (h o)", h=HALVES))
+        nc.sync.dma_start(wbw[:].bitcast(I32), wb_words[0].bitcast(I32))
+        load_scale_rows(nc.sync, wbs, wb_scales)
+        nc.sync.dma_start(slot_list[:], offs2)
+        nc.sync.dma_start(page_list[:], offs4)
+
+        xg = tile("xg", [P, J], U16)
+        xsg = tile("xsg", [P, J], U8)
+        nc.vector.tensor_copy(xg[:], xw[:].indirect(tok_list[:]))
+        nc.vector.tensor_copy(xsg[:], xs[:].indirect(tok_list[:]))
+
+        wp = tile("wp", [P, PACK, P], U32)
+        wsp = tile("wsp", [P, PACK, P], U8)
+        w2p = tile("w2p", [P, PACK, P], U32)
+        w2sp = tile("w2sp", [P, PACK, P], U8)
+        nc.scalar.copy(wp[:].rearrange("p t m -> p m t"), ww[:].rearrange("p (m t) -> p m t", t=PACK))
+
+        def deal_scales(dealt, plane):
+            words = plane[:].bitcast(I32)
+            nc.vector.tensor_copy(words[64:128, 0 : R // 4], words[0:64, R // 4 : R // 2])
+            nc.vector.tensor_copy(dealt[:], plane[:, 0:R].rearrange("p (m t) -> p t m", t=PACK))
+
+        deal_scales(wsp, ws)
+        nc.scalar.copy(w2p[:].rearrange("p t m -> p m t"), w2w[:].rearrange("p (m t) -> p m t", t=PACK))
+        deal_scales(w2sp, w2s)
+
+        def first_stage(name, words, scales, fmt, jh):
+            bank = ps.tile([P, PACK, SLOTS], F32, name=name)
+            cols = slice(SLOTS * jh, SLOTS * (jh + 1))
+            for t in range(PACK):
+                nc.tensor.matmul_mx(
+                    bank[:, t, :],
+                    lhsT=words[:, t, :].bitcast(fmt),
+                    lhsT_scale=scales[:, t, :],
+                    rhs=xg[:, cols].bitcast(E2M1X4),
+                    rhs_scale=xsg[:, cols],
+                    start=True,
+                    stop=True,
+                )
+            return bank
+
+        a_bank = [first_stage("a%d" % jh, wp, wsp, E4M3X4, jh) for jh in range(HALVES)]
+        b_bank = [first_stage("b%d" % jh, w2p, w2sp, E5M2X4, jh) for jh in range(HALVES)]
+        a_sb = [tile("a_sb%d" % jh, [P, SLOTS, PACK], F32) for jh in range(HALVES)]
+        for jh in range(HALVES):
+            nc.scalar.copy(a_sb[jh][:], a_bank[jh][:].rearrange("p t j -> p j t"))
+
+        gain = []
+        for h in range(HALVES):
+            codes = tile("gain_codes%d" % h, [P, U], U8)
+            nc.vector.tensor_copy(codes[:], store[h][:].indirect(gain_list[:]))
+            g = tile("gain%d" % h, [P, U], F32)
+            nc.scalar.activation(g[:], codes[:].bitcast(E4M3), COPY, scale=step[:, h : h + 1])
+            gain.append(g)
+
+        p_sb = [tile("p_sb%d" % h, [P, J], F32) for h in range(HALVES)]
+        hid = tile("hid", [P, HALVES, SLOTS, PACK], BF16, tag="store1")
+        for jh in range(HALVES):
+            nc.vector.tensor_tensor(hid[:, jh], a_sb[jh][:], b_bank[jh][:].rearrange("p t j -> p j t"), MAX)
+        for jh in range(HALVES):
+            hq = tile("hq%d" % jh, [P, SLOTS], U32)
+            hs = tile("hs%d" % jh, [P, SLOTS], U8)
+            nc.vector.quantize_mx(hq[:].bitcast(E5M2X4), hs[:], hid[:, jh].rearrange("p j t -> p (j t)"))
+            for h in range(HALVES):
+                bank = ps.tile([P, SLOTS], F32, name="p%d%d" % (jh, h))
+                rows = slice(P * h, P * (h + 1))
+                nc.tensor.matmul_mx(
+                    bank[:],
+                    lhsT=wbw[:, rows].bitcast(E2M1X4),
+                    lhsT_scale=wbs[:, rows],
+                    rhs=hq[:].bitcast(E5M2X4),
+                    rhs_scale=hs[:],
+                    start=True,
+                    stop=True,
+                )
+                dst = p_sb[h][:, SLOTS * jh : SLOTS * (jh + 1)]
+                if h == 0:
+                    nc.vector.tensor_copy(dst, bank[:])
+                else:
+                    nc.scalar.copy(dst, bank[:])
+
+        ends0 = tile("ends0", [P, U], F32)
+        picked1 = tile("picked1", [P, U], F32)
+        nc.vector.tensor_tensor(ends0[:], p_sb[0][:].indirect(slot_list[:]), gain[0][:], MULT)
+        nc.scalar.activation(picked1[:], p_sb[1][:].indirect(slot_list[:]), COPY)
+        nc.vector.tensor_tensor(page[1][:].indirect(page_list[:]), picked1[:], gain[1][:], MULT)
+        nc.scalar.activation(page[0][:].indirect(page_list[:]), ends0[:], COPY)
+        nc.scalar.dma_start(out[0:P, :], page[0][:])
+        nc.sync.dma_start(out[P : 2 * P, :], page[1][:])

@@ -28,8 +28,8 @@ SLOTS = 128
 HALVES = 2
 
 
-def load_scale_rows(queue, plane, scales):
-    for q in range(QUADS):
+def load_scale_rows(queue, plane, scales, quads):
+    for q in quads:
         queue.dma_start(
             plane[QUAD * q : QUAD * q + ROWS, :].bitcast(I32),
             scales[0, ROWS * q : ROWS * (q + 1), :].bitcast(I32),
@@ -69,27 +69,29 @@ def tile_list_outcomegain_kernel(
         for h in range(HALVES):
             nc.vector.memset(page[h][:], 0.0)
 
-        def load_folded(plane, scales):
+        def load_folded(queue, plane, scales, q):
             rows = scales[0].bitcast(I32).rearrange("(u q r) c -> q r u c", u=2, q=2)
-            for q in range(2):
-                nc.sync.dma_start(
-                    plane[:].bitcast(I32)[QUAD * q : QUAD * q + ROWS, :].rearrange("r (u c) -> r u c", u=2), rows[q]
-                )
+            queue.dma_start(
+                plane[:].bitcast(I32)[QUAD * q : QUAD * q + ROWS, :].rearrange("r (u c) -> r u c", u=2), rows[q]
+            )
 
-        load_scale_rows(nc.scalar, xs, xt_scales)
         nc.sync.dma_start(tok_list[:], offs)
-        nc.sync.dma_start(xw[:].bitcast(I32), xt_words[0].bitcast(I32))
-        nc.sync.dma_start(ww[:].bitcast(I32), w_words[0].rearrange("p c t -> p (c t)").bitcast(I32))
-        load_folded(ws, w_scales)
+        nc.scalar.dma_start(xw[:].bitcast(I32), xt_words[0].bitcast(I32))
+        load_scale_rows(nc.sync, xs, xt_scales, (0, 2))
+        load_scale_rows(nc.scalar, xs, xt_scales, (1, 3))
+        load_folded(nc.sync, ws, w_scales, 0)
+        nc.scalar.dma_start(ww[:].bitcast(I32), w_words[0].rearrange("p c t -> p (c t)").bitcast(I32))
+        load_folded(nc.scalar, ws, w_scales, 1)
         nc.sync.dma_start(w2w[:].bitcast(I32), w2_words[0].rearrange("p c t -> p (c t)").bitcast(I32))
-        load_folded(w2s, w2_scales)
+        load_folded(nc.sync, w2s, w2_scales, 0)
+        load_folded(nc.sync, w2s, w2_scales, 1)
         nc.sync.dma_start(gain_list[:], offs3)
         for h in range(HALVES):
             nc.sync.dma_start(store[h][:], ca[P * h : P * (h + 1), :])
         with nc.allow_non_contiguous_dma(reason="one float32 step for each partition and half"):
             nc.sync.dma_start(step[:], sz.rearrange("(h p) o -> p (h o)", h=HALVES))
         nc.sync.dma_start(wbw[:].bitcast(I32), wb_words[0].bitcast(I32))
-        load_scale_rows(nc.sync, wbs, wb_scales)
+        load_scale_rows(nc.sync, wbs, wb_scales, range(QUADS))
         nc.sync.dma_start(slot_list[:], offs2)
         nc.sync.dma_start(page_list[:], offs4)
 
@@ -102,15 +104,24 @@ def tile_list_outcomegain_kernel(
         wsp = tile("wsp", [P, PACK, P], U8)
         w2p = tile("w2p", [P, PACK, P], U32)
         w2sp = tile("w2sp", [P, PACK, P], U8)
-        nc.scalar.copy(wp[:].rearrange("p t m -> p m t"), ww[:].rearrange("p (m t) -> p m t", t=PACK))
+
+        def deal_words(dealt, words):
+            nc.scalar.copy(
+                dealt[:].rearrange("p t (c i) -> p c t i", i=2),
+                words[:].rearrange("p (c i t) -> p c t i", i=2, t=PACK),
+            )
+
+        deal_words(wp, ww)
 
         def deal_scales(dealt, plane):
             words = plane[:].bitcast(I32)
             nc.vector.tensor_copy(words[64:128, 0 : R // 4], words[0:64, R // 4 : R // 2])
-            nc.vector.tensor_copy(dealt[:], plane[:, 0:R].rearrange("p (m t) -> p t m", t=PACK))
+            by_slab = plane[:, 0:R].rearrange("p (m t) -> p t m", t=PACK)
+            for t in range(0, PACK, 2):
+                nc.vector.tensor_copy(dealt[:, t : t + 2, :], by_slab[:, t : t + 2, :])
 
         deal_scales(wsp, ws)
-        nc.scalar.copy(w2p[:].rearrange("p t m -> p m t"), w2w[:].rearrange("p (m t) -> p m t", t=PACK))
+        deal_words(w2p, w2w)
         deal_scales(w2sp, w2s)
 
         def first_stage(name, words, scales, fmt, jh):
@@ -150,7 +161,7 @@ def tile_list_outcomegain_kernel(
             hq = tile("hq%d" % jh, [P, SLOTS], U32)
             hs = tile("hs%d" % jh, [P, SLOTS], U8)
             nc.vector.quantize_mx(hq[:].bitcast(E5M2X4), hs[:], hid[:, jh].rearrange("p j t -> p (j t)"))
-            for h in range(HALVES):
+            for h in reversed(range(HALVES)):
                 bank = ps.tile([P, SLOTS], F32, name="p%d%d" % (jh, h))
                 rows = slice(P * h, P * (h + 1))
                 nc.tensor.matmul_mx(

@@ -141,9 +141,9 @@ def tile_list_outcomegain_kernel(
 
         a_bank = [first_stage("a%d" % jh, wp, wsp, E4M3X4, jh) for jh in range(HALVES)]
         b_bank = [first_stage("b%d" % jh, w2p, w2sp, E5M2X4, jh) for jh in range(HALVES)]
-        a_sb = [tile("a_sb%d" % jh, [P, SLOTS, PACK], F32) for jh in range(HALVES)]
+        a_sb = [tile("a_sb%d" % jh, [P, SLOTS // 2, PACK, 2], F32) for jh in range(HALVES)]
         for jh in range(HALVES):
-            nc.scalar.copy(a_sb[jh][:], a_bank[jh][:].rearrange("p t j -> p j t"))
+            nc.scalar.copy(a_sb[jh][:], a_bank[jh][:].rearrange("p t (c i) -> p c t i", i=2))
 
         gain = []
         for h in range(HALVES):
@@ -156,7 +156,12 @@ def tile_list_outcomegain_kernel(
         p_sb = [tile("p_sb%d" % h, [P, J], F32) for h in range(HALVES)]
         hid = tile("hid", [P, HALVES, SLOTS, PACK], BF16, tag="store1")
         for jh in range(HALVES):
-            nc.vector.tensor_tensor(hid[:, jh], a_sb[jh][:], b_bank[jh][:].rearrange("p t j -> p j t"), MAX)
+            nc.vector.tensor_tensor(
+                hid[:, jh].rearrange("p (c i) t -> p c t i", i=2),
+                a_sb[jh][:],
+                b_bank[jh][:].rearrange("p t (c i) -> p c t i", i=2),
+                MAX,
+            )
         for jh in range(HALVES):
             hq = tile("hq%d" % jh, [P, SLOTS], U32)
             hs = tile("hs%d" % jh, [P, SLOTS], U8)

@@ -55,7 +55,8 @@ def tile_list_outcomegain_kernel(
         xw = tile("xw", [P, T], U16)
         xs = tile("xs", [P, T], U8)
         ww = tile("ww", [P, R], U32)
-        ws = tile("ws", [P, 2 * R], U8)
+        ws = tile("ws", [P, R], U8)
+        ws_rows = tile("ws_rows", [ROWS, QUADS, R // 4], I32)
         w2w = tile("w2w", [P, R], U32)
         w2s = tile("w2s", [P, 2 * R], U8)
         wbw = tile("wbw", [P, N], U16)
@@ -75,14 +76,13 @@ def tile_list_outcomegain_kernel(
                 plane[:].bitcast(I32)[QUAD * q : QUAD * q + ROWS, :].rearrange("r (u c) -> r u c", u=2), rows[q]
             )
 
-        nc.sync.dma_start(tok_list[:], offs)
+        nc.sync.dma_start(ws_rows[:], w_scales[0].bitcast(I32).rearrange("(q r) c -> r q c", q=QUADS))
         nc.scalar.dma_start(xw[:].bitcast(I32), xt_words[0].bitcast(I32))
-        load_scale_rows(nc.sync, xs, xt_scales, (0, 2))
+        nc.sync.dma_start(tok_list[:], offs)
         load_scale_rows(nc.scalar, xs, xt_scales, (1, 3))
-        load_folded(nc.sync, ws, w_scales, 0)
+        load_scale_rows(nc.sync, xs, xt_scales, (0, 2))
         nc.scalar.dma_start(ww[:].bitcast(I32), w_words[0].rearrange("p c t -> p (c t)").bitcast(I32))
-        load_folded(nc.scalar, ws, w_scales, 1)
-        nc.sync.dma_start(w2w[:].bitcast(I32), w2_words[0].rearrange("p c t -> p (c t)").bitcast(I32))
+        nc.scalar.dma_start(w2w[:].bitcast(I32), w2_words[0].rearrange("p c t -> p (c t)").bitcast(I32))
         load_folded(nc.sync, w2s, w2_scales, 0)
         load_folded(nc.sync, w2s, w2_scales, 1)
         nc.sync.dma_start(gain_list[:], offs3)
@@ -96,9 +96,10 @@ def tile_list_outcomegain_kernel(
         nc.sync.dma_start(page_list[:], offs4)
 
         xg = tile("xg", [P, J], U16)
-        xsg = tile("xsg", [P, J], U8)
+        xsg = [tile("xsg%d" % jh, [P, SLOTS], U8) for jh in range(HALVES)]
+        for q in range(QUADS):
+            nc.vector.tensor_copy(ws[:].bitcast(I32)[QUAD * q : QUAD * q + ROWS, :], ws_rows[:, q, :])
         nc.vector.tensor_copy(xg[:], xw[:].indirect(tok_list[:]))
-        nc.vector.tensor_copy(xsg[:], xs[:].indirect(tok_list[:]))
 
         wp = tile("wp", [P, PACK, P], U32)
         wsp = tile("wsp", [P, PACK, P], U8)
@@ -106,22 +107,25 @@ def tile_list_outcomegain_kernel(
         w2sp = tile("w2sp", [P, PACK, P], U8)
 
         def deal_words(dealt, words):
-            nc.scalar.copy(
-                dealt[:].rearrange("p t (c i) -> p c t i", i=2),
-                words[:].rearrange("p (c i t) -> p c t i", i=2, t=PACK),
-            )
+            dst = dealt[:].rearrange("p t (c i) -> p c t i", i=2)
+            src = words[:].rearrange("p (c i t) -> p c t i", i=2, t=PACK)
+            for t in range(0, PACK, 2):
+                nc.scalar.copy(dst[:, :, t : t + 2, :], src[:, :, t : t + 2, :])
 
         deal_words(wp, ww)
 
         def deal_scales(dealt, plane):
-            words = plane[:].bitcast(I32)
-            nc.vector.tensor_copy(words[64:128, 0 : R // 4], words[0:64, R // 4 : R // 2])
             by_slab = plane[:, 0:R].rearrange("p (m t) -> p t m", t=PACK)
             for t in range(0, PACK, 2):
                 nc.vector.tensor_copy(dealt[:, t : t + 2, :], by_slab[:, t : t + 2, :])
 
         deal_scales(wsp, ws)
+        for jh in range(HALVES):
+            entries = tok_list[:, SLOTS // 16 * jh : SLOTS // 16 * (jh + 1)]
+            nc.vector.tensor_copy(xsg[jh][:], xs[:].indirect(entries))
         deal_words(w2p, w2w)
+        w2s_words = w2s[:].bitcast(I32)
+        nc.vector.tensor_copy(w2s_words[64:128, 0 : R // 4], w2s_words[0:64, R // 4 : R // 2])
         deal_scales(w2sp, w2s)
 
         def first_stage(name, words, scales, fmt, jh):
@@ -133,7 +137,7 @@ def tile_list_outcomegain_kernel(
                     lhsT=words[:, t, :].bitcast(fmt),
                     lhsT_scale=scales[:, t, :],
                     rhs=xg[:, cols].bitcast(E2M1X4),
-                    rhs_scale=xsg[:, cols],
+                    rhs_scale=xsg[jh][:],
                     start=True,
                     stop=True,
                 )
@@ -166,7 +170,7 @@ def tile_list_outcomegain_kernel(
             hq = tile("hq%d" % jh, [P, SLOTS], U32)
             hs = tile("hs%d" % jh, [P, SLOTS], U8)
             nc.vector.quantize_mx(hq[:].bitcast(E5M2X4), hs[:], hid[:, jh].rearrange("p j t -> p (j t)"))
-            for h in reversed(range(HALVES)):
+            for h in range(HALVES):
                 bank = ps.tile([P, SLOTS], F32, name="p%d%d" % (jh, h))
                 rows = slice(P * h, P * (h + 1))
                 nc.tensor.matmul_mx(

from contextlib import ExitStack

import concourse.mybir as mybir

K, T, J, R, U, V, E, N = 512, 1024, 256, 512, 128, 1024, 512, 256
FLOPS = 2 * (2 * K * R * J + R * N * J)

F32 = mybir.dt.float32
BF16 = mybir.dt.bfloat16
I32 = mybir.dt.int32
U32 = mybir.dt.uint32
U16 = mybir.dt.uint16
U8 = mybir.dt.uint8
E4M3 = mybir.dt.float8_e4m3fn
E4M3X4 = mybir.dt.float8_e4m3fn_x4
E5M2X4 = mybir.dt.float8_e5m2_x4
E2M1X4 = mybir.dt.float4_e2m1fn_x4
MULT = mybir.AluOpType.mult
MAX = mybir.AluOpType.max
COPY = mybir.ActivationFunctionType.Copy

P = 128
PACK = 4
QUADS = 4
QUAD = 32
ROWS = 4
SLOTS = 128
HALVES = 2


def load_scale_rows(queue, plane, scales, quads):
    for q in quads:
        queue.dma_start(
            plane[QUAD * q : QUAD * q + ROWS, :].bitcast(I32),
            scales[0, ROWS * q : ROWS * (q + 1), :].bitcast(I32),
        )


def tile_list_outcomegain_kernel(
    tc, xt_words, xt_scales, w_words, w_scales, w2_words, w2_scales, wb_words, wb_scales,
    ca, sz, offs, offs2, offs3, offs4, out,
):
    nc = tc.nc
    with ExitStack() as ctx:
        sb = ctx.enter_context(tc.tile_pool(name="sb", bufs=1))
        ps = ctx.enter_context(tc.psum_pool(name="ps", bufs=1))

        def tile(name, shape, dtype, tag=None):
            return sb.tile(shape, dtype, name=name, tag=tag or name, align_bytes=64)

        tok_list = tile("tok_list", [P, J // 16], U16)
        slot_list = tile("slot_list", [P, U // 16], U16)
        gain_list = tile("gain_list", [P, U // 16], U16)
        page_list = tile("page_list", [P, U // 16], U16)
        xw = tile("xw", [P, T], U16)
        xs = tile("xs", [P, T], U8)
        ww = tile("ww", [P, R], U32)
        ws = tile("ws", [P, R], U8)
        ws_rows = tile("ws_rows", [ROWS, QUADS, R // 4], I32)
        w2w = tile("w2w", [P, R], U32)
        w2s = tile("w2s", [P, 2 * R], U8)
        wbw = tile("wbw", [P, N], U16)
        wbs = tile("wbs", [P, N], U8)
        step = tile("step", [P, HALVES], F32)
        store = [tile("store%d" % h, [P, V], U8) for h in range(HALVES)]
        page = [tile("page%d" % h, [P, E], F32) for h in range(HALVES)]

        for plane in (xs, ws, w2s, wbs):
            nc.vector.memset(plane[:].bitcast(I32), 0)
        for h in range(HALVES):
            nc.vector.memset(page[h][:], 0.0)

        def load_folded(queue, plane, scales, q):
            rows = scales[0].bitcast(I32).rearrange("(u q r) c -> q r u c", u=2, q=2)
            queue.dma_start(
                plane[:].bitcast(I32)[QUAD * q : QUAD * q + ROWS, :].rearrange("r (u c) -> r u c", u=2), rows[q]
            )

        nc.sync.dma_start(ws_rows[:], w_scales[0].bitcast(I32).rearrange("(q r) c -> r q c", q=QUADS))
        nc.scalar.dma_start(xw[:].bitcast(I32), xt_words[0].bitcast(I32))
        nc.sync.dma_start(tok_list[:], offs)
        load_scale_rows(nc.scalar, xs, xt_scales, (1, 3))
        load_scale_rows(nc.sync, xs, xt_scales, (0, 2))
        nc.scalar.dma_start(ww[:].bitcast(I32), w_words[0].rearrange("p c t -> p (c t)").bitcast(I32))
        nc.scalar.dma_start(w2w[:].bitcast(I32), w2_words[0].rearrange("p c t -> p (c t)").bitcast(I32))
        load_folded(nc.sync, w2s, w2_scales, 0)
        load_folded(nc.sync, w2s, w2_scales, 1)
        nc.sync.dma_start(gain_list[:], offs3)
        for h in range(HALVES):
            nc.sync.dma_start(store[h][:], ca[P * h : P * (h + 1), :])
        with nc.allow_non_contiguous_dma(reason="one float32 step for each partition and half"):
            nc.sync.dma_start(step[:], sz.rearrange("(h p) o -> p (h o)", h=HALVES))
        nc.sync.dma_start(wbw[:].bitcast(I32), wb_words[0].bitcast(I32))
        load_scale_rows(nc.sync, wbs, wb_scales, range(QUADS))
        nc.sync.dma_start(slot_list[:], offs2)
        nc.sync.dma_start(page_list[:], offs4)

        xg = tile("xg", [P, J], U16)
        xsg = [tile("xsg%d" % jh, [P, SLOTS], U8) for jh in range(HALVES)]
        for q in range(QUADS):
            nc.vector.tensor_copy(ws[:].bitcast(I32)[QUAD * q : QUAD * q + ROWS, :], ws_rows[:, q, :])
        nc.vector.tensor_copy(xg[:], xw[:].indirect(tok_list[:]))

        wp = tile("wp", [P, PACK, P], U32)
        wsp = tile("wsp", [P, PACK, P], U8)
        w2p = tile("w2p", [P, PACK, P], U32)
        w2sp = tile("w2sp", [P, PACK, P], U8)

        def deal_words(dealt, words):
            dst = dealt[:].rearrange("p t (c i) -> p c t i", i=2)
            src = words[:].rearrange("p (c i t) -> p c t i", i=2, t=PACK)
            for t in range(0, PACK, 2):
                nc.scalar.copy(dst[:, :, t : t + 2, :], src[:, :, t : t + 2, :])

        deal_words(wp, ww)

        def deal_scales(dealt, plane):
            by_slab = plane[:, 0:R].rearrange("p (m t) -> p t m", t=PACK)
            for t in range(0, PACK, 2):
                nc.vector.tensor_copy(dealt[:, t : t + 2, :], by_slab[:, t : t + 2, :])

        deal_scales(wsp, ws)
        for jh in range(HALVES):
            entries = tok_list[:, SLOTS // 16 * jh : SLOTS // 16 * (jh + 1)]
            nc.vector.tensor_copy(xsg[jh][:], xs[:].indirect(entries))
        deal_words(w2p, w2w)
        w2s_words = w2s[:].bitcast(I32)
        nc.vector.tensor_copy(w2s_words[64:128, 0 : R // 4], w2s_words[0:64, R // 4 : R // 2])
        deal_scales(w2sp, w2s)

        def first_stage(name, words, scales, fmt, jh):
            bank = ps.tile([P, PACK, SLOTS], F32, name=name)
            cols = slice(SLOTS * jh, SLOTS * (jh + 1))
            for t in range(PACK):
                nc.tensor.matmul_mx(
                    bank[:, t, :],
                    lhsT=words[:, t, :].bitcast(fmt),
                    lhsT_scale=scales[:, t, :],
                    rhs=xg[:, cols].bitcast(E2M1X4),
                    rhs_scale=xsg[jh][:],
                    start=True,
                    stop=True,
                )
            return bank

        a_bank = [first_stage("a%d" % jh, wp, wsp, E4M3X4, jh) for jh in range(HALVES)]
        b_bank = [first_stage("b%d" % jh, w2p, w2sp, E5M2X4, jh) for jh in range(HALVES)]
        a_sb = [tile("a_sb%d" % jh, [P, SLOTS // 2, PACK, 2], F32) for jh in range(HALVES)]
        for jh in range(HALVES):
            nc.scalar.copy(a_sb[jh][:], a_bank[jh][:].rearrange("p t (c i) -> p c t i", i=2))

        gain = []
        for h in range(HALVES):
            codes = tile("gain_codes%d" % h, [P, U], U8)
            nc.vector.tensor_copy(codes[:], store[h][:].indirect(gain_list[:]))
            g = tile("gain%d" % h, [P, U], F32)
            nc.scalar.activation(g[:], codes[:].bitcast(E4M3), COPY, scale=step[:, h : h + 1])
            gain.append(g)

        p_sb = [tile("p_sb%d" % h, [P, J], F32) for h in range(HALVES)]
        hid = tile("hid", [P, HALVES, SLOTS, PACK], BF16, tag="store1")
        for jh in range(HALVES):
            nc.vector.tensor_tensor(
                hid[:, jh].rearrange("p (c i) t -> p c t i", i=2),
                a_sb[jh][:],
                b_bank[jh][:].rearrange("p t (c i) -> p c t i", i=2),
                MAX,
            )
        for jh in range(HALVES):
            hq = tile("hq%d" % jh, [P, SLOTS], U32)
            hs = tile("hs%d" % jh, [P, SLOTS], U8)
            nc.vector.quantize_mx(hq[:].bitcast(E5M2X4), hs[:], hid[:, jh].rearrange("p j t -> p (j t)"))
            for h in range(HALVES):
                bank = ps.tile([P, SLOTS], F32, name="p%d%d" % (jh, h))
                rows = slice(P * h, P * (h + 1))
                nc.tensor.matmul_mx(
                    bank[:],
                    lhsT=wbw[:, rows].bitcast(E2M1X4),
                    lhsT_scale=wbs[:, rows],
                    rhs=hq[:].bitcast(E5M2X4),
                    rhs_scale=hs[:],
                    start=True,
                    stop=True,
                )
                dst = p_sb[h][:, SLOTS * jh : SLOTS * (jh + 1)]
                if h == 0:
                    nc.vector.tensor_copy(dst, bank[:])
                else:
                    nc.scalar.copy(dst, bank[:])

        ends0 = tile("ends0", [P, U], F32)
        picked1 = tile("picked1", [P, U], F32)
        nc.vector.tensor_tensor(ends0[:], p_sb[0][:].indirect(slot_list[:]), gain[0][:], MULT)
        nc.scalar.activation(picked1[:], p_sb[1][:].indirect(slot_list[:]), COPY)
        nc.vector.tensor_tensor(page[1][:].indirect(page_list[:]), picked1[:], gain[1][:], MULT)
        nc.scalar.activation(page[0][:].indirect(page_list[:]), ends0[:], COPY)
        nc.scalar.dma_start(out[0:P, :], page[0][:])
        nc.sync.dma_start(out[P : 2 * P, :], page[1][:])
